import numpy as np
import ml_dtypes


def mxq(x, axis, fmt="e4m3"):
    dtype, down = {"e4m3": (ml_dtypes.float8_e4m3fn, 7), "e5m2": (ml_dtypes.float8_e5m2, 14)}[fmt]
    v = np.moveaxis(np.asarray(x, np.float32).astype(ml_dtypes.bfloat16).astype(np.float64), axis, -1)
    blocks = v.reshape(v.shape[:-1] + (-1, 32))
    amax = np.abs(blocks).max(-1, keepdims=True)
    byte = np.maximum(np.where(amax > 0, np.frexp(amax)[1] - 1 + 127, 0) - down, 1)
    scale = np.exp2(byte - 127.0)
    codes = (blocks / scale).astype(np.float32).astype(dtype).astype(np.float64)
    return np.moveaxis((codes * scale).reshape(v.shape), -1, axis)


WIDE = False


def mx_kscale(k):
    if not WIDE:
        return np.ones(k)
    levels = np.array([10, -10, 5, -5, 0])
    if k % 512:
        return np.exp2(np.random.permutation(np.resize(levels, k // 32))).repeat(32)
    a = np.empty((k // 512, 16))
    for p in range(k // 512):
        a[p, :8] = np.random.permutation(np.resize(levels, 8))
        for g in range(8):
            far = levels[np.abs(levels - a[p, g]) >= 10]
            a[p, g + 8] = far[np.random.randint(len(far))]
    return np.exp2(a.ravel()).repeat(32)


def f64(x):
    return np.asarray(x).astype(np.float64)


def striped(idx):
    return np.tile(idx.reshape(-1, 16).T, (8, 1)).astype(np.uint16)


def unstriped(offs):
    return offs[:16].T.reshape(-1).astype(np.int64)


E2M1 = np.array([0.0, 0.5, 1.0, 1.5, 2.0, 3.0, 4.0, 6.0, -0.0, -0.5, -1.0, -1.5, -2.0, -3.0, -4.0, -6.0])


def pack_weight(w, fmt):
    k, n = w.shape
    w = f64(np.asarray(w, np.float32).astype(ml_dtypes.bfloat16)).reshape(k // 32, 32, n)
    amax = np.abs(w).max(1)
    if fmt == "e4m3":
        byte = np.frexp(amax)[1] - 1 + 127 - 7
    else:
        mant, ex = np.frexp(amax / 6.0)
        byte = np.where(mant > 0.5, ex, ex - 1) + 127
    byte = np.clip(np.where(amax > 0, byte, 1), 1, 254)
    scaled = (w * np.exp2(127.0 - byte)[:, None, :]).reshape(k, n).astype(np.float32)
    by_word = np.ascontiguousarray(scaled.reshape(k // 512, 128, 4, n).transpose(0, 1, 3, 2))
    if fmt == "e4m3":
        words = by_word.astype(ml_dtypes.float8_e4m3fn).view(np.uint8)
    else:
        c = by_word.astype(ml_dtypes.float4_e2m1fn).view(np.uint8) & 0xF
        words = (c[..., 0::2] | (c[..., 1::2] << 4)).reshape(k // 512, 128, 2 * n)
    return np.ascontiguousarray(words), np.ascontiguousarray(byte.astype(np.uint8).reshape(k // 512, 16, n))


def unpack_weight(words, scales, fmt):
    g, _, n = scales.shape
    words = np.ascontiguousarray(words).reshape(g, 128, n, -1)
    if fmt == "e4m3":
        vals = words.view(ml_dtypes.float8_e4m3fn).astype(np.float64)
    else:
        nib = np.empty((g, 128, n, 4), np.uint8)
        nib[..., 0::2] = words & 0xF
        nib[..., 1::2] = words >> 4
        vals = E2M1[nib]
    vals = vals * np.repeat(np.exp2(scales.astype(np.float64) - 127.0), 8, axis=1)[..., None]
    return vals.transpose(0, 1, 3, 2).reshape(g * 512, n)


K, T, E, C, N = 768, 640, 5, 256, 512


def by_expert(wq, xq):
    return np.concatenate([wq[e].T @ xq[:, e * C:(e + 1) * C] for e in range(E)], axis=1)


def setup_inputs():
    n = np.random.standard_normal
    s = mx_kscale(N)[:, None]
    first = np.random.permutation(np.repeat(np.arange(E), T // E))
    second = (first + 1 + np.random.permutation(np.repeat(np.arange(E - 1), -(-T // (E - 1)))[:T])) % E
    while np.bincount(second, minlength=E).max() != T // E:
        load = np.bincount(second, minlength=E); hi, lo = int(load.argmax()), int(load.argmin())
        t = np.flatnonzero((second == hi) & (first != lo))[0]; second[t] = lo
    slot_token = np.empty(E * C, np.int64); pos = np.empty((2, T), np.int64); fill = np.zeros(E, np.int64)
    place = np.stack([np.random.permutation(C) for _ in range(E)])
    for r, deal in enumerate((first, second)):
        for t in np.random.permutation(T):
            e = deal[t]; j = e * C + place[e, fill[e]]; fill[e] += 1; slot_token[j] = t; pos[r, t] = j
    g = np.random.uniform(0.2, 0.8, T)
    w_slot = np.empty(E * C); w_slot[pos[0]] = g; w_slot[pos[1]] = 1.0 - g
    dy = pack_weight(n((N, T)) * s, "e4m3")
    return {
        "dy_words": dy[0],
        "dy_scales": dy[1],
        "w": (n((E, N, K)) / np.sqrt(N) / s[None]).astype(np.float32),
        "gate": np.tile(w_slot, (K, 1)).astype(np.float32),
        "offs": striped(slot_token),
        "pos1": striped(pos[0]),
        "pos2": striped(pos[1]),
    }


def reference(dy_words, dy_scales, w, gate, offs, pos1, pos2):
    idx = unstriped(offs)
    gq = unpack_weight(dy_words, dy_scales, "e4m3")[:, idx]
    dx = f64(gate) * by_expert(mxq(f64(w), 1, "e4m3"), gq)
    return dx[:, unstriped(pos1)] + dx[:, unstriped(pos2)]

@@ -1,0 +1,155 @@
+from contextlib import ExitStack
+
+import concourse.mybir as mybir
+from concourse.masks import make_identity
+
+K, T, E, C, N = 768, 640, 5, 256, 512
+S = E * C
+P = 128
+PACK = 4
+WIN = 2048
+FLOPS = 2 * N * K * S
+BYTES = 4 * E * N * K + N * T + 16 * T + 4 * S + 4 * K * T + 2 * 128 * 160
+
+F32 = mybir.dt.float32
+BF16 = mybir.dt.bfloat16
+I32 = mybir.dt.int32
+U32 = mybir.dt.uint32
+U16 = mybir.dt.uint16
+U8 = mybir.dt.uint8
+FP8X4 = mybir.dt.float8_e4m3fn_x4
+COPY = mybir.ActivationFunctionType.Copy
+MULT = mybir.AluOpType.mult
+ADD = mybir.AluOpType.add
+
+CHUNKS = ((128, 0), (256, 0), (384, 4))
+HOLD = {"first1": "grouped2_3", "both1": "grouped2_4"}
+GATE_AFTER = (1, 1)
+
+
+def pieces(kw):
+    return [(0, kw)] if kw != 384 else [(0, 256), (256, 384)]
+
+
+def tile_moe_bdx_lin_none_kernel(tc, dy_words, dy_scales, w, gate, offs, pos1, pos2, out):
+    nc = tc.nc
+    with ExitStack() as ctx:
+        lists = ctx.enter_context(tc.tile_pool(name="lists", bufs=1))
+        keep = ctx.enter_context(tc.tile_pool(name="keep", bufs=1))
+        psum = ctx.enter_context(tc.psum_pool(name="psum", bufs=1))
+
+        offs_sb = lists.tile([P, S // 16], U16, name="offs_sb")
+        pos1_sb = lists.tile([P, T // 16], U16, name="pos1_sb")
+        pos2_sb = lists.tile([P, T // 16], U16, name="pos2_sb")
+        dy_w = keep.tile([P, WIN], I32, name="dy_w")
+        dy_s = keep.tile([P, WIN], U8, name="dy_s")
+        gate_rows = keep.tile([P, S], F32, name="gate_rows")
+        gate_cols = keep.tile([P, S // P], F32, name="gate_cols")
+        ident = keep.tile([P, P], F32, name="ident")
+
+        nc.vector.memset(dy_s[:].bitcast(I32), 0)
+        nc.vector.memset(dy_w[:, T:WIN], 0)
+        nc.sync.dma_start(dy_w[:, 0:T], dy_words[0].rearrange("p t d -> p (t d)").bitcast(I32))
+        nc.sync.dma_start(offs_sb[:], offs)
+        make_identity(nc, ident[:])
+
+        raw = {}
+        k0 = 0
+        last = len(CHUNKS) - 1
+        for ci, (kw, nt) in enumerate(CHUNKS):
+            for e in range(E):
+                raw[ci, e] = keep.tile([P, PACK, kw], F32, name=f"raw{ci}_{e}", tag=f"raw{ci}_{e}")
+                nc.sync.dma_start(raw[ci, e][:], w[e, :, k0 : k0 + kw].rearrange("(p j) k -> p j k", j=PACK))
+                if (ci, e) == (0, 2):
+                    for q in range(4):
+                        nc.sync.dma_start(dy_s[32 * q : 32 * q + 4, 0:T].bitcast(I32), dy_scales[0, 4 * q : 4 * q + 4, :].bitcast(I32))
+                if (ci, e) == GATE_AFTER:
+                    nc.sync.dma_start(gate_rows[:], gate[0:P, :])
+                    nc.sync.dma_start(pos1_sb[:], pos1)
+                    nc.sync.dma_start(pos2_sb[:], pos2)
+                if (ci, e) == (last, 0):
+                    with nc.allow_non_contiguous_dma(reason="one gate value a partition"):
+                        nc.sync.dma_start(gate_cols[:], gate[0, :].rearrange("(c p) -> p c", p=P))
+            k0 = k0 + kw
+
+        g_w = []
+        g_s = []
+        codes = {}
+        scales = {}
+
+        gw = keep.tile([P, S], U32, name="g_w", align_bytes=64)
+        gs = keep.tile([P, S], U8, name="g_s", align_bytes=64)
+        nc.vector.tensor_copy(gw[:], dy_w[:].bitcast(U32).indirect(offs_sb[:]))
+        nc.vector.tensor_copy(gs[:], dy_s[:].indirect(offs_sb[:]))
+        for e in range(E):
+            g_w.append(gw[:, e * C : (e + 1) * C])
+            g_s.append(gs[:, e * C : (e + 1) * C])
+
+        def cast_quant(ci, e):
+            kw = CHUNKS[ci][0]
+            grouped = keep.tile([P, kw, PACK], BF16, name=f"grouped{ci}_{e}", tag=f"grouped{ci}_{e}", align_bytes=64)
+            nc.scalar.activation(
+                grouped[:].rearrange("p (c i) t -> p c t i", i=4),
+                raw[ci, e][:].rearrange("p t (c i) -> p c t i", i=4),
+                COPY,
+            )
+            codes[ci, e] = keep.tile([P, kw], U32, name=f"codes{ci}_{e}", align_bytes=64)
+            scales[ci, e] = keep.tile([P, kw], U8, name=f"scales{ci}_{e}", align_bytes=64)
+            for a, b in pieces(kw):
+                nc.vector.quantize_mx(
+                    out=codes[ci, e][:, a:b].bitcast(FP8X4),
+                    scales=scales[ci, e][:, a:b],
+                    in_=grouped[:, a:b, :].rearrange("p k t -> p (k t)"),
+                )
+
+        def mm(dst, lw, ls, rw, rs):
+            nc.tensor.matmul_mx(out=dst, lhsT=lw.bitcast(FP8X4), lhsT_scale=ls, rhs=rw.bitcast(FP8X4), rhs_scale=rs, start=True, stop=True)
+
+        def products(ci, dx):
+            kw, nt = CHUNKS[ci]
+            nb = kw // P
+            nd = E - nt
+            for e0 in range(0, nd, 2):
+                es = list(range(e0, min(e0 + 2, nd)))
+                for b in range(nb):
+                    bank = psum.tile([P, 512], F32, name="direct", bufs=3)
+                    for e in es:
+                        c0 = (e - e0) * C
+                        mm(bank[:, c0 : c0 + C], codes[ci, e][:, b * P : (b + 1) * P], scales[ci, e][:, b * P : (b + 1) * P], g_w[e], g_s[e])
+                    cols = slice(e0 * C, (e0 + len(es)) * C)
+                    nc.vector.tensor_tensor(dx[b][:, cols], bank[:, 0 : len(es) * C], gate_rows[:, cols], MULT)
+            if nt:
+                staged = keep.tile([P, 2 * nt, kw], F32, name=f"staged{ci}", tag=f"raw{ci}_{E - 1}")
+            for sb in range(2 * nt):
+                e, h = divmod(2 * nd + sb, 2)
+                bank = psum.tile([P, 512], F32, name="turned", bufs=3)
+                for a, b in pieces(kw):
+                    mm(bank[:, a:b], g_w[e][:, h * P : (h + 1) * P], g_s[e][:, h * P : (h + 1) * P], codes[ci, e][:, a:b], scales[ci, e][:, a:b])
+                nc.scalar.activation(staged[:, sb, :], bank[:, 0:kw], COPY, scale=gate_cols[:, 2 * nd + sb : 2 * nd + sb + 1])
+            for b in range(nb):
+                for s0 in range(0, 2 * nt, 4):
+                    s1 = min(s0 + 4, 2 * nt)
+                    back = psum.tile([P, 512], F32, name="back", bufs=2)
+                    for sb in range(s0, s1):
+                        nc.tensor.transpose(back[:, (sb - s0) * P : (sb - s0 + 1) * P], staged[:, sb, b * P : (b + 1) * P], ident[:])
+                    nc.scalar.copy(dx[b][:, (2 * nd + s0) * P : (2 * nd + s1) * P], back[:, 0 : (s1 - s0) * P])
+
+        def combine(kb, dxb):
+            first = keep.tile([P, T], F32, name=f"first{kb}", tag=HOLD.get(f"first{kb}", f"first{kb}"), align_bytes=64)
+            nc.vector.tensor_copy(first[:], dxb[:].indirect(pos1_sb[:]))
+            both = keep.tile([P, T], F32, name=f"both{kb}", tag=HOLD.get(f"both{kb}", f"both{kb}"), align_bytes=64)
+            nc.vector.tensor_tensor(both[:], dxb[:].indirect(pos2_sb[:]), first[:], ADD)
+            nc.sync.dma_start(out[kb * P : (kb + 1) * P, :], both[:])
+
+        for e in range(E):
+            cast_quant(0, e)
+        kb = 0
+        for ci, (kw, nt) in enumerate(CHUNKS):
+            dx = [keep.tile([P, S], F32, name=f"dx{kb + b}") for b in range(kw // P)]
+            products(ci, dx)
+            if ci < last:
+                for e in range(E):
+                    cast_quant(ci + 1, e)
+            for b in range(kw // P):
+                combine(kb + b, dx[b])
+            kb = kb + kw // P

@@ -7,7 +7,8 @@ K, T, E, C, N = 768, 640, 5, 256, 512
 S = E * C
 P = 128
 PACK = 4
-WIN = 2048
+WIN = 1728
+WIN_S = 704
 FLOPS = 2 * N * K * S
 BYTES = 4 * E * N * K + N * T + 16 * T + 4 * S + 4 * K * T + 2 * 128 * 160
 
@@ -22,13 +23,15 @@ COPY = mybir.ActivationFunctionType.Copy
 MULT = mybir.AluOpType.mult
 ADD = mybir.AluOpType.add
 
-CHUNKS = ((128, 0), (256, 0), (384, 4))
-HOLD = {"first1": "grouped2_3", "both1": "grouped2_4"}
-GATE_AFTER = (1, 1)
+CHUNKS = ((128, 0), (256, 0), (384, 5))
+HOLD = {"dx1": "grouped1_3", "dx2": "grouped1_4", "first1": "grouped2_2", "first2": "grouped2_3", "late1": "grouped2_4", "staged2": "raw2_4"}
+GROUPS = (((0, 1), (2, 3), (4,)), ((0, 1), (2, 3), (4,)), ((0, 1), (2,), (3,), (4,)))
+GATE_AFTER = (0, 4)
 
 
 def pieces(kw):
-    return [(0, kw)] if kw != 384 else [(0, 256), (256, 384)]
+    top = max(x for x in (128, 256, 512) if x <= kw)
+    return [(0, kw)] if kw == top else [(0, top), (top, kw)]
 
 
 def tile_moe_bdx_lin_none_kernel(tc, dy_words, dy_scales, w, gate, offs, pos1, pos2, out):
@@ -42,9 +45,8 @@ def tile_moe_bdx_lin_none_kernel(tc, dy_words, dy_scales, w, gate, offs, pos1, p
         pos1_sb = lists.tile([P, T // 16], U16, name="pos1_sb")
         pos2_sb = lists.tile([P, T // 16], U16, name="pos2_sb")
         dy_w = keep.tile([P, WIN], I32, name="dy_w")
-        dy_s = keep.tile([P, WIN], U8, name="dy_s")
+        dy_s = keep.tile([P, WIN_S], U8, name="dy_s")
         gate_rows = keep.tile([P, S], F32, name="gate_rows")
-        gate_cols = keep.tile([P, S // P], F32, name="gate_cols")
         ident = keep.tile([P, P], F32, name="ident")
 
         nc.vector.memset(dy_s[:].bitcast(I32), 0)
@@ -67,9 +69,6 @@ def tile_moe_bdx_lin_none_kernel(tc, dy_words, dy_scales, w, gate, offs, pos1, p
                     nc.sync.dma_start(gate_rows[:], gate[0:P, :])
                     nc.sync.dma_start(pos1_sb[:], pos1)
                     nc.sync.dma_start(pos2_sb[:], pos2)
-                if (ci, e) == (last, 0):
-                    with nc.allow_non_contiguous_dma(reason="one gate value a partition"):
-                        nc.sync.dma_start(gate_cols[:], gate[0, :].rearrange("(c p) -> p c", p=P))
             k0 = k0 + kw
 
         g_w = []
@@ -80,25 +79,32 @@ def tile_moe_bdx_lin_none_kernel(tc, dy_words, dy_scales, w, gate, offs, pos1, p
         gw = keep.tile([P, S], U32, name="g_w", align_bytes=64)
         gs = keep.tile([P, S], U8, name="g_s", align_bytes=64)
         nc.vector.tensor_copy(gw[:], dy_w[:].bitcast(U32).indirect(offs_sb[:]))
-        nc.vector.tensor_copy(gs[:], dy_s[:].indirect(offs_sb[:]))
+        for es in GROUPS[0]:
+            s0, s1 = es[0] * C, (es[-1] + 1) * C
+            nc.vector.tensor_copy(gs[:, s0:s1], dy_s[:].indirect(offs_sb[:, s0 // 16 : s1 // 16]))
         for e in range(E):
             g_w.append(gw[:, e * C : (e + 1) * C])
             g_s.append(gs[:, e * C : (e + 1) * C])
 
-        def cast_quant(ci, e):
+        def cast_quant(ci, es):
             kw = CHUNKS[ci][0]
-            grouped = keep.tile([P, kw, PACK], BF16, name=f"grouped{ci}_{e}", tag=f"grouped{ci}_{e}", align_bytes=64)
-            nc.scalar.activation(
-                grouped[:].rearrange("p (c i) t -> p c t i", i=4),
-                raw[ci, e][:].rearrange("p t (c i) -> p c t i", i=4),
-                COPY,
-            )
-            codes[ci, e] = keep.tile([P, kw], U32, name=f"codes{ci}_{e}", align_bytes=64)
-            scales[ci, e] = keep.tile([P, kw], U8, name=f"scales{ci}_{e}", align_bytes=64)
-            for a, b in pieces(kw):
+            width = len(es) * kw
+            grouped = keep.tile([P, width, PACK], BF16, name=f"grouped{ci}_{es[-1]}", tag=f"grouped{ci}_{es[-1]}", align_bytes=64)
+            cw = keep.tile([P, width], U32, name=f"codes{ci}_{es[-1]}", align_bytes=64)
+            cs = keep.tile([P, width], U8, name=f"scales{ci}_{es[-1]}", align_bytes=64)
+            for n, e in enumerate(es):
+                cols = slice(n * kw, (n + 1) * kw)
+                nc.scalar.activation(
+                    grouped[:, cols, :].rearrange("p (c i) t -> p c t i", i=4),
+                    raw[ci, e][:].rearrange("p t (c i) -> p c t i", i=4),
+                    COPY,
+                )
+                codes[ci, e] = cw[:, cols]
+                scales[ci, e] = cs[:, cols]
+            for a, b in pieces(width):
                 nc.vector.quantize_mx(
-                    out=codes[ci, e][:, a:b].bitcast(FP8X4),
-                    scales=scales[ci, e][:, a:b],
+                    out=cw[:, a:b].bitcast(FP8X4),
+                    scales=cs[:, a:b],
                     in_=grouped[:, a:b, :].rearrange("p k t -> p (k t)"),
                 )
 
@@ -112,44 +118,63 @@ def tile_moe_bdx_lin_none_kernel(tc, dy_words, dy_scales, w, gate, offs, pos1, p
             for e0 in range(0, nd, 2):
                 es = list(range(e0, min(e0 + 2, nd)))
                 for b in range(nb):
-                    bank = psum.tile([P, 512], F32, name="direct", bufs=3)
+                    bank = psum.tile([P, 512], F32, name="bank", bufs=8)
                     for e in es:
                         c0 = (e - e0) * C
                         mm(bank[:, c0 : c0 + C], codes[ci, e][:, b * P : (b + 1) * P], scales[ci, e][:, b * P : (b + 1) * P], g_w[e], g_s[e])
                     cols = slice(e0 * C, (e0 + len(es)) * C)
                     nc.vector.tensor_tensor(dx[b][:, cols], bank[:, 0 : len(es) * C], gate_rows[:, cols], MULT)
             if nt:
-                staged = keep.tile([P, 2 * nt, kw], F32, name=f"staged{ci}", tag=f"raw{ci}_{E - 1}")
-            for sb in range(2 * nt):
-                e, h = divmod(2 * nd + sb, 2)
-                bank = psum.tile([P, 512], F32, name="turned", bufs=3)
-                for a, b in pieces(kw):
-                    mm(bank[:, a:b], g_w[e][:, h * P : (h + 1) * P], g_s[e][:, h * P : (h + 1) * P], codes[ci, e][:, a:b], scales[ci, e][:, a:b])
-                nc.scalar.activation(staged[:, sb, :], bank[:, 0:kw], COPY, scale=gate_cols[:, 2 * nd + sb : 2 * nd + sb + 1])
+                gate_cols = keep.tile([P, S // P], F32, name="gate_cols", tag=f"raw{ci}_{E - 2}")
+            for s0 in range(0, 2 * nt, 4):
+                s1 = min(s0 + 4, 2 * nt)
+                turned_gate = psum.tile([P, 4, P], F32, name="bank", bufs=8)
+                for sb in range(s0, s1):
+                    c0 = (2 * nd + sb) * P
+                    nc.tensor.transpose(turned_gate[:, sb - s0, :], gate_rows[:, c0 : c0 + P], ident[:])
+                nc.scalar.copy(gate_cols[:, 2 * nd + s0 : 2 * nd + s1], turned_gate[:, 0 : s1 - s0, 0])
+            if nt:
+                staged = keep.tile([P, nb, 2 * nt, P], F32, name=f"staged{ci}", tag=HOLD.get(f"staged{ci}", f"staged{ci}"))
             for b in range(nb):
                 for s0 in range(0, 2 * nt, 4):
                     s1 = min(s0 + 4, 2 * nt)
-                    back = psum.tile([P, 512], F32, name="back", bufs=2)
+                    bank = psum.tile([P, 4, P], F32, name="bank", bufs=8)
                     for sb in range(s0, s1):
-                        nc.tensor.transpose(back[:, (sb - s0) * P : (sb - s0 + 1) * P], staged[:, sb, b * P : (b + 1) * P], ident[:])
+                        e, h = divmod(2 * nd + sb, 2)
+                        mm(bank[:, sb - s0, :], g_w[e][:, h * P : (h + 1) * P], g_s[e][:, h * P : (h + 1) * P], codes[ci, e][:, b * P : (b + 1) * P], scales[ci, e][:, b * P : (b + 1) * P])
+                    for sb in range(s0, s1):
+                        nc.scalar.activation(staged[:, b, sb, :], bank[:, sb - s0, :], COPY, scale=gate_cols[:, 2 * nd + sb : 2 * nd + sb + 1])
+                for s0 in range(0, 2 * nt, 4):
+                    s1 = min(s0 + 4, 2 * nt)
+                    back = psum.tile([P, 512], F32, name="bank", bufs=8)
+                    for sb in range(s0, s1):
+                        nc.tensor.transpose(back[:, (sb - s0) * P : (sb - s0 + 1) * P], staged[:, b, sb, :], ident[:])
                     nc.scalar.copy(dx[b][:, (2 * nd + s0) * P : (2 * nd + s1) * P], back[:, 0 : (s1 - s0) * P])
 
-        def combine(kb, dxb):
-            first = keep.tile([P, T], F32, name=f"first{kb}", tag=HOLD.get(f"first{kb}", f"first{kb}"), align_bytes=64)
-            nc.vector.tensor_copy(first[:], dxb[:].indirect(pos1_sb[:]))
-            both = keep.tile([P, T], F32, name=f"both{kb}", tag=HOLD.get(f"both{kb}", f"both{kb}"), align_bytes=64)
-            nc.vector.tensor_tensor(both[:], dxb[:].indirect(pos2_sb[:]), first[:], ADD)
-            nc.sync.dma_start(out[kb * P : (kb + 1) * P, :], both[:])
+        def combine(ci, kb, dx):
+            nb = len(dx)
+            first = []
+            for b in range(nb):
+                one = keep.tile([P, T], F32, name=f"first{kb + b}", tag=HOLD.get(f"first{kb + b}", f"first{kb + b}"), align_bytes=64)
+                nc.vector.tensor_copy(one[:], dx[b][:].indirect(pos1_sb[:]))
+                first.append(one)
+            late = keep.tile([P, nb, T], F32, name=f"late{ci}", tag=HOLD.get(f"late{ci}", f"late{ci}"), align_bytes=64)
+            for b in range(nb):
+                parts = 2 if kb + b == K // P - 1 else 1
+                tw = T // parts
+                for part in range(parts):
+                    toks = slice(part * tw, (part + 1) * tw)
+                    nc.vector.tensor_tensor(late[:, b, toks], dx[b][:].indirect(pos2_sb[:, part * tw // 16 : (part + 1) * tw // 16]), first[b][:, toks], ADD)
+                    nc.sync.dma_start(out[(kb + b) * P : (kb + b + 1) * P, toks], late[:, b, toks])
 
-        for e in range(E):
-            cast_quant(0, e)
+        for es in GROUPS[0]:
+            cast_quant(0, es)
         kb = 0
         for ci, (kw, nt) in enumerate(CHUNKS):
-            dx = [keep.tile([P, S], F32, name=f"dx{kb + b}") for b in range(kw // P)]
+            dx = [keep.tile([P, S], F32, name=f"dx{kb + b}", tag=HOLD.get(f"dx{kb + b}", f"dx{kb + b}"), align_bytes=64) for b in range(kw // P)]
             products(ci, dx)
             if ci < last:
-                for e in range(E):
-                    cast_quant(ci + 1, e)
-            for b in range(kw // P):
-                combine(kb + b, dx[b])
+                for es in GROUPS[ci + 1]:
+                    cast_quant(ci + 1, es)
+            combine(ci, kb, dx)
             kb = kb + kw // P

@@ -7,10 +7,12 @@ K, T, E, C, N = 768, 640, 5, 256, 512
 S = E * C
 P = 128
 PACK = 4
-WIN = 1728
-WIN_S = 704
+PER_COL = 16
+BANK = 512
+PER_BANK = BANK // P
+SLOT_BLOCKS = S // P
 FLOPS = 2 * N * K * S
-BYTES = 4 * E * N * K + N * T + 16 * T + 4 * S + 4 * K * T + 2 * 128 * 160
+BYTES = 4 * E * N * K + N * T + (N // 32) * T + 4 * S + 4 * K * T + 2 * P * (S + 2 * T) // PER_COL
 
 F32 = mybir.dt.float32
 BF16 = mybir.dt.bfloat16
@@ -23,15 +25,32 @@ COPY = mybir.ActivationFunctionType.Copy
 MULT = mybir.AluOpType.mult
 ADD = mybir.AluOpType.add
 
-CHUNKS = ((128, 0), (256, 0), (384, 5))
-HOLD = {"dx1": "grouped1_3", "dx2": "grouped1_4", "first1": "grouped2_2", "first2": "grouped2_3", "late1": "grouped2_4", "staged2": "raw2_4"}
-GROUPS = (((0, 1), (2, 3), (4,)), ((0, 1), (2, 3), (4,)), ((0, 1), (2,), (3,), (4,)))
-GATE_AFTER = (0, 4)
+CHUNKS = (128, 256, 384)
+MIDDLE = 1
+LAST = 2
+PAIRS = ((0, 1), (2, 3), (4,))
+GROUPS = (PAIRS, PAIRS, ((0, 1), (2,), (3,), (4,)))
+WORD_WINDOW = 1728
+BYTE_WINDOW = 704
 
 
-def pieces(kw):
-    top = max(x for x in (128, 256, 512) if x <= kw)
-    return [(0, kw)] if kw == top else [(0, top), (top, kw)]
+def quantise_pieces(width):
+    top = max(piece for piece in (128, 256, 512) if piece <= width)
+    return [(0, width)] if width == top else [(0, top), (top, width)]
+
+
+def raw_tag(chunk, e):
+    return f"raw{chunk}_{e}"
+
+
+TAKES_OVER = {
+    "dx1": raw_tag(MIDDLE, 3),
+    "dx2": raw_tag(MIDDLE, 4),
+    "gate_cols": raw_tag(LAST, 1),
+    "first1": raw_tag(LAST, 2),
+    "first2": raw_tag(LAST, 3),
+    "after_rounding": raw_tag(LAST, 4),
+}
 
 
 def tile_moe_bdx_lin_none_kernel(tc, dy_words, dy_scales, w, gate, offs, pos1, pos2, out):
@@ -41,140 +60,169 @@ def tile_moe_bdx_lin_none_kernel(tc, dy_words, dy_scales, w, gate, offs, pos1, p
         keep = ctx.enter_context(tc.tile_pool(name="keep", bufs=1))
         psum = ctx.enter_context(tc.psum_pool(name="psum", bufs=1))
 
-        offs_sb = lists.tile([P, S // 16], U16, name="offs_sb")
-        pos1_sb = lists.tile([P, T // 16], U16, name="pos1_sb")
-        pos2_sb = lists.tile([P, T // 16], U16, name="pos2_sb")
-        dy_w = keep.tile([P, WIN], I32, name="dy_w")
-        dy_s = keep.tile([P, WIN_S], U8, name="dy_s")
+        def sbuf(name, shape, dtype):
+            return keep.tile(shape, dtype, name=name, tag=TAKES_OVER.get(name, name), align_bytes=64)
+
+        def next_bank(shape):
+            return psum.tile(shape, F32, name="bank", bufs=8)
+
+        def block(b):
+            return slice(b * P, (b + 1) * P)
+
+        def slots(e_first, e_last):
+            return slice(e_first * C, (e_last + 1) * C)
+
+        def entries(list_tile, span):
+            return list_tile[:, span.start // PER_COL : span.stop // PER_COL]
+
+        offs_sb = lists.tile([P, S // PER_COL], U16, name="offs_sb")
+        pos1_sb = lists.tile([P, T // PER_COL], U16, name="pos1_sb")
+        pos2_sb = lists.tile([P, T // PER_COL], U16, name="pos2_sb")
+        dy_w = keep.tile([P, WORD_WINDOW], I32, name="dy_w")
+        dy_s = keep.tile([P, BYTE_WINDOW], U8, name="dy_s")
         gate_rows = keep.tile([P, S], F32, name="gate_rows")
         ident = keep.tile([P, P], F32, name="ident")
 
         nc.vector.memset(dy_s[:].bitcast(I32), 0)
-        nc.vector.memset(dy_w[:, T:WIN], 0)
+        nc.vector.memset(dy_w[:, T:WORD_WINDOW], 0)
         nc.sync.dma_start(dy_w[:, 0:T], dy_words[0].rearrange("p t d -> p (t d)").bitcast(I32))
         nc.sync.dma_start(offs_sb[:], offs)
         make_identity(nc, ident[:])
 
         raw = {}
-        k0 = 0
-        last = len(CHUNKS) - 1
-        for ci, (kw, nt) in enumerate(CHUNKS):
-            for e in range(E):
-                raw[ci, e] = keep.tile([P, PACK, kw], F32, name=f"raw{ci}_{e}", tag=f"raw{ci}_{e}")
-                nc.sync.dma_start(raw[ci, e][:], w[e, :, k0 : k0 + kw].rearrange("(p j) k -> p j k", j=PACK))
-                if (ci, e) == (0, 2):
-                    for q in range(4):
-                        nc.sync.dma_start(dy_s[32 * q : 32 * q + 4, 0:T].bitcast(I32), dy_scales[0, 4 * q : 4 * q + 4, :].bitcast(I32))
-                if (ci, e) == GATE_AFTER:
-                    nc.sync.dma_start(gate_rows[:], gate[0:P, :])
-                    nc.sync.dma_start(pos1_sb[:], pos1)
-                    nc.sync.dma_start(pos2_sb[:], pos2)
-            k0 = k0 + kw
 
-        g_w = []
-        g_s = []
+        def load_w(chunk, experts):
+            k0 = sum(CHUNKS[:chunk])
+            for e in experts:
+                raw[chunk, e] = sbuf(raw_tag(chunk, e), [P, PACK, CHUNKS[chunk]], F32)
+                rows = w[e, :, k0 : k0 + CHUNKS[chunk]]
+                nc.sync.dma_start(raw[chunk, e][:], rows.rearrange("(p j) k -> p j k", j=PACK))
+
+        load_w(0, range(0, 3))
+        for q in range(4):
+            nc.sync.dma_start(dy_s[32 * q : 32 * q + 4, 0:T].bitcast(I32), dy_scales[0, 4 * q : 4 * q + 4, :].bitcast(I32))
+        load_w(0, range(3, E))
+        nc.sync.dma_start(gate_rows[:], gate[0:P, :])
+        nc.sync.dma_start(pos1_sb[:], pos1)
+        nc.sync.dma_start(pos2_sb[:], pos2)
+        for chunk in range(1, len(CHUNKS)):
+            load_w(chunk, range(E))
+
+        g_w = keep.tile([P, S], U32, name="g_w", align_bytes=64)
+        g_s = keep.tile([P, S], U8, name="g_s", align_bytes=64)
+        nc.vector.tensor_copy(g_w[:], dy_w[:].bitcast(U32).indirect(offs_sb[:]))
+        for experts in PAIRS:
+            cols = slots(experts[0], experts[-1])
+            nc.vector.tensor_copy(g_s[:, cols], dy_s[:].indirect(entries(offs_sb, cols)))
+
         codes = {}
         scales = {}
 
-        gw = keep.tile([P, S], U32, name="g_w", align_bytes=64)
-        gs = keep.tile([P, S], U8, name="g_s", align_bytes=64)
-        nc.vector.tensor_copy(gw[:], dy_w[:].bitcast(U32).indirect(offs_sb[:]))
-        for es in GROUPS[0]:
-            s0, s1 = es[0] * C, (es[-1] + 1) * C
-            nc.vector.tensor_copy(gs[:, s0:s1], dy_s[:].indirect(offs_sb[:, s0 // 16 : s1 // 16]))
-        for e in range(E):
-            g_w.append(gw[:, e * C : (e + 1) * C])
-            g_s.append(gs[:, e * C : (e + 1) * C])
-
-        def cast_quant(ci, es):
-            kw = CHUNKS[ci][0]
-            width = len(es) * kw
-            grouped = keep.tile([P, width, PACK], BF16, name=f"grouped{ci}_{es[-1]}", tag=f"grouped{ci}_{es[-1]}", align_bytes=64)
-            cw = keep.tile([P, width], U32, name=f"codes{ci}_{es[-1]}", align_bytes=64)
-            cs = keep.tile([P, width], U8, name=f"scales{ci}_{es[-1]}", align_bytes=64)
-            for n, e in enumerate(es):
-                cols = slice(n * kw, (n + 1) * kw)
+        def round_and_quantise(chunk, experts):
+            kw = CHUNKS[chunk]
+            width = len(experts) * kw
+            rounded = sbuf(f"rounded{chunk}_{experts[-1]}", [P, width, PACK], BF16)
+            words = sbuf(f"codes{chunk}_{experts[-1]}", [P, width], U32)
+            plane = sbuf(f"scales{chunk}_{experts[-1]}", [P, width], U8)
+            for place, e in enumerate(experts):
+                cols = slice(place * kw, (place + 1) * kw)
                 nc.scalar.activation(
-                    grouped[:, cols, :].rearrange("p (c i) t -> p c t i", i=4),
-                    raw[ci, e][:].rearrange("p t (c i) -> p c t i", i=4),
+                    rounded[:, cols, :].rearrange("p (c i) t -> p c t i", i=4),
+                    raw[chunk, e][:].rearrange("p t (c i) -> p c t i", i=4),
                     COPY,
                 )
-                codes[ci, e] = cw[:, cols]
-                scales[ci, e] = cs[:, cols]
-            for a, b in pieces(width):
+                codes[chunk, e] = words[:, cols]
+                scales[chunk, e] = plane[:, cols]
+            for lo, hi in quantise_pieces(width):
                 nc.vector.quantize_mx(
-                    out=cw[:, a:b].bitcast(FP8X4),
-                    scales=cs[:, a:b],
-                    in_=grouped[:, a:b, :].rearrange("p k t -> p (k t)"),
+                    out=words[:, lo:hi].bitcast(FP8X4),
+                    scales=plane[:, lo:hi],
+                    in_=rounded[:, lo:hi, :].rearrange("p k t -> p (k t)"),
                 )
 
-        def mm(dst, lw, ls, rw, rs):
-            nc.tensor.matmul_mx(out=dst, lhsT=lw.bitcast(FP8X4), lhsT_scale=ls, rhs=rw.bitcast(FP8X4), rhs_scale=rs, start=True, stop=True)
+        def product(dst, still_words, still_scales, moving_words, moving_scales):
+            nc.tensor.matmul_mx(
+                out=dst,
+                lhsT=still_words.bitcast(FP8X4),
+                lhsT_scale=still_scales,
+                rhs=moving_words.bitcast(FP8X4),
+                rhs_scale=moving_scales,
+                start=True,
+                stop=True,
+            )
 
-        def products(ci, dx):
-            kw, nt = CHUNKS[ci]
-            nb = kw // P
-            nd = E - nt
-            for e0 in range(0, nd, 2):
-                es = list(range(e0, min(e0 + 2, nd)))
-                for b in range(nb):
-                    bank = psum.tile([P, 512], F32, name="bank", bufs=8)
-                    for e in es:
-                        c0 = (e - e0) * C
-                        mm(bank[:, c0 : c0 + C], codes[ci, e][:, b * P : (b + 1) * P], scales[ci, e][:, b * P : (b + 1) * P], g_w[e], g_s[e])
-                    cols = slice(e0 * C, (e0 + len(es)) * C)
-                    nc.vector.tensor_tensor(dx[b][:, cols], bank[:, 0 : len(es) * C], gate_rows[:, cols], MULT)
-            if nt:
-                gate_cols = keep.tile([P, S // P], F32, name="gate_cols", tag=f"raw{ci}_{E - 2}")
-            for s0 in range(0, 2 * nt, 4):
-                s1 = min(s0 + 4, 2 * nt)
-                turned_gate = psum.tile([P, 4, P], F32, name="bank", bufs=8)
-                for sb in range(s0, s1):
-                    c0 = (2 * nd + sb) * P
-                    nc.tensor.transpose(turned_gate[:, sb - s0, :], gate_rows[:, c0 : c0 + P], ident[:])
-                nc.scalar.copy(gate_cols[:, 2 * nd + s0 : 2 * nd + s1], turned_gate[:, 0 : s1 - s0, 0])
-            if nt:
-                staged = keep.tile([P, nb, 2 * nt, P], F32, name=f"staged{ci}", tag=HOLD.get(f"staged{ci}", f"staged{ci}"))
-            for b in range(nb):
-                for s0 in range(0, 2 * nt, 4):
-                    s1 = min(s0 + 4, 2 * nt)
-                    bank = psum.tile([P, 4, P], F32, name="bank", bufs=8)
-                    for sb in range(s0, s1):
-                        e, h = divmod(2 * nd + sb, 2)
-                        mm(bank[:, sb - s0, :], g_w[e][:, h * P : (h + 1) * P], g_s[e][:, h * P : (h + 1) * P], codes[ci, e][:, b * P : (b + 1) * P], scales[ci, e][:, b * P : (b + 1) * P])
-                    for sb in range(s0, s1):
-                        nc.scalar.activation(staged[:, b, sb, :], bank[:, sb - s0, :], COPY, scale=gate_cols[:, 2 * nd + sb : 2 * nd + sb + 1])
-                for s0 in range(0, 2 * nt, 4):
-                    s1 = min(s0 + 4, 2 * nt)
-                    back = psum.tile([P, 512], F32, name="bank", bufs=8)
-                    for sb in range(s0, s1):
-                        nc.tensor.transpose(back[:, (sb - s0) * P : (sb - s0 + 1) * P], staged[:, b, sb, :], ident[:])
-                    nc.scalar.copy(dx[b][:, (2 * nd + s0) * P : (2 * nd + s1) * P], back[:, 0 : (s1 - s0) * P])
+        def direct_chunk(chunk, dx):
+            for experts in PAIRS:
+                cols = slots(experts[0], experts[-1])
+                for b in range(len(dx)):
+                    bank = next_bank([P, BANK])
+                    for place, e in enumerate(experts):
+                        product(bank[:, slots(place, place)], codes[chunk, e][:, block(b)], scales[chunk, e][:, block(b)], g_w[:, slots(e, e)], g_s[:, slots(e, e)])
+                    nc.vector.tensor_tensor(dx[b][:, cols], bank[:, 0 : len(experts) * C], gate_rows[:, cols], MULT)
 
-        def combine(ci, kb, dx):
-            nb = len(dx)
+        def turned_chunk(dx, scaled):
+            fills = [range(lo, min(lo + PER_BANK, SLOT_BLOCKS)) for lo in range(0, SLOT_BLOCKS, PER_BANK)]
+            gate_cols = sbuf("gate_cols", [P, SLOT_BLOCKS], F32)
+            for fill in fills:
+                bank = next_bank([P, PER_BANK, P])
+                for j in fill:
+                    nc.tensor.transpose(bank[:, j - fill.start, :], gate_rows[:, block(j)], ident[:])
+                nc.scalar.copy(gate_cols[:, fill.start : fill.stop], bank[:, 0 : len(fill), 0])
+            for b in range(len(dx)):
+                for fill in fills:
+                    bank = next_bank([P, PER_BANK, P])
+                    for j in fill:
+                        e = j * P // C
+                        product(bank[:, j - fill.start, :], g_w[:, block(j)], g_s[:, block(j)], codes[LAST, e][:, block(b)], scales[LAST, e][:, block(b)])
+                    for j in fill:
+                        nc.scalar.activation(scaled[:, b, j, :], bank[:, j - fill.start, :], COPY, scale=gate_cols[:, j : j + 1])
+                for fill in fills:
+                    bank = next_bank([P, BANK])
+                    for j in fill:
+                        nc.tensor.transpose(bank[:, block(j - fill.start)], scaled[:, b, j, :], ident[:])
+                    nc.scalar.copy(dx[b][:, fill.start * P : fill.stop * P], bank[:, 0 : len(fill) * P])
+
+        def combine(chunk, first_block, dx, sums):
+            parts = 1 if chunk == MIDDLE else 2
+            halves = [slice(part * T // parts, (part + 1) * T // parts) for part in range(parts)]
             first = []
-            for b in range(nb):
-                one = keep.tile([P, T], F32, name=f"first{kb + b}", tag=HOLD.get(f"first{kb + b}", f"first{kb + b}"), align_bytes=64)
-                nc.vector.tensor_copy(one[:], dx[b][:].indirect(pos1_sb[:]))
-                first.append(one)
-            late = keep.tile([P, nb, T], F32, name=f"late{ci}", tag=HOLD.get(f"late{ci}", f"late{ci}"), align_bytes=64)
-            for b in range(nb):
-                parts = 2 if kb + b == K // P - 1 else 1
-                tw = T // parts
-                for part in range(parts):
-                    toks = slice(part * tw, (part + 1) * tw)
-                    nc.vector.tensor_tensor(late[:, b, toks], dx[b][:].indirect(pos2_sb[:, part * tw // 16 : (part + 1) * tw // 16]), first[b][:, toks], ADD)
-                    nc.sync.dma_start(out[(kb + b) * P : (kb + b + 1) * P, toks], late[:, b, toks])
+            for b in range(len(dx)):
+                picked = sbuf(f"first{first_block + b}", [P, T], F32)
+                for toks in halves:
+                    nc.vector.tensor_copy(picked[:, toks], dx[b][:].indirect(entries(pos1_sb, toks)))
+                first.append(picked)
+            for b in range(len(dx)):
+                rows = block(first_block + b)
+                is_final = rows.stop == K
+                for toks in halves:
+                    nc.vector.tensor_tensor(sums[:, b, toks], dx[b][:].indirect(entries(pos2_sb, toks)), first[b][:, toks], ADD)
+                    if is_final:
+                        nc.sync.dma_start(out[rows, toks], sums[:, b, toks])
+                if not is_final:
+                    nc.sync.dma_start(out[rows, :], sums[:, b, :])
 
-        for es in GROUPS[0]:
-            cast_quant(0, es)
-        kb = 0
-        for ci, (kw, nt) in enumerate(CHUNKS):
-            dx = [keep.tile([P, S], F32, name=f"dx{kb + b}", tag=HOLD.get(f"dx{kb + b}", f"dx{kb + b}"), align_bytes=64) for b in range(kw // P)]
-            products(ci, dx)
-            if ci < last:
-                for es in GROUPS[ci + 1]:
-                    cast_quant(ci + 1, es)
-            combine(ci, kb, dx)
-            kb = kb + kw // P
+        def chunk_results(chunk):
+            first_block = sum(CHUNKS[:chunk]) // P
+            return first_block, [sbuf(f"dx{first_block + b}", [P, S], F32) for b in range(CHUNKS[chunk] // P)]
+
+        for experts in GROUPS[0]:
+            round_and_quantise(0, experts)
+
+        first_block, dx = chunk_results(0)
+        direct_chunk(0, dx)
+        for experts in GROUPS[MIDDLE]:
+            round_and_quantise(MIDDLE, experts)
+        combine(0, first_block, dx, sbuf("sums0", [P, len(dx), T], F32))
+
+        first_block, dx = chunk_results(MIDDLE)
+        direct_chunk(MIDDLE, dx)
+        for experts in GROUPS[LAST]:
+            round_and_quantise(LAST, experts)
+        sums_cols = len(dx) * T
+        scaled_cols = (CHUNKS[LAST] // P) * S
+        after_rounding = sbuf("after_rounding", [P, sums_cols + scaled_cols], F32)
+        combine(MIDDLE, first_block, dx, after_rounding[:, 0:sums_cols].rearrange("p (b t) -> p b t", t=T))
+
+        first_block, dx = chunk_results(LAST)
+        turned_chunk(dx, after_rounding[:, sums_cols : sums_cols + scaled_cols].rearrange("p (b j k) -> p b j k", j=SLOT_BLOCKS, k=P))
+        combine(LAST, first_block, dx, sbuf("sums2", [P, len(dx), T], F32))

from contextlib import ExitStack

import concourse.mybir as mybir
from concourse.masks import make_identity

K, T, E, C, N = 768, 640, 5, 256, 512
S = E * C
P = 128
PACK = 4
PER_COL = 16
BANK = 512
PER_BANK = BANK // P
SLOT_BLOCKS = S // P
FLOPS = 2 * N * K * S
BYTES = 4 * E * N * K + N * T + (N // 32) * T + 4 * S + 4 * K * T + 2 * P * (S + 2 * T) // PER_COL

F32 = mybir.dt.float32
BF16 = mybir.dt.bfloat16
I32 = mybir.dt.int32
U32 = mybir.dt.uint32
U16 = mybir.dt.uint16
U8 = mybir.dt.uint8
FP8X4 = mybir.dt.float8_e4m3fn_x4
COPY = mybir.ActivationFunctionType.Copy
MULT = mybir.AluOpType.mult
ADD = mybir.AluOpType.add

CHUNKS = (128, 256, 384)
MIDDLE = 1
LAST = 2
PAIRS = ((0, 1), (2, 3), (4,))
GROUPS = (PAIRS, PAIRS, ((0, 1), (2,), (3,), (4,)))
WORD_WINDOW = 1728
BYTE_WINDOW = 704


def quantise_pieces(width):
    top = max(piece for piece in (128, 256, 512) if piece <= width)
    return [(0, width)] if width == top else [(0, top), (top, width)]


def raw_tag(chunk, e):
    return f"raw{chunk}_{e}"


TAKES_OVER = {
    "dx1": raw_tag(MIDDLE, 3),
    "dx2": raw_tag(MIDDLE, 4),
    "gate_cols": raw_tag(LAST, 1),
    "first1": raw_tag(LAST, 2),
    "first2": raw_tag(LAST, 3),
    "after_rounding": raw_tag(LAST, 4),
}


def tile_moe_bdx_lin_none_kernel(tc, dy_words, dy_scales, w, gate, offs, pos1, pos2, out):
    nc = tc.nc
    with ExitStack() as ctx:
        lists = ctx.enter_context(tc.tile_pool(name="lists", bufs=1))
        keep = ctx.enter_context(tc.tile_pool(name="keep", bufs=1))
        psum = ctx.enter_context(tc.psum_pool(name="psum", bufs=1))

        def sbuf(name, shape, dtype):
            return keep.tile(shape, dtype, name=name, tag=TAKES_OVER.get(name, name), align_bytes=64)

        def next_bank(shape):
            return psum.tile(shape, F32, name="bank", bufs=8)

        def block(b):
            return slice(b * P, (b + 1) * P)

        def slots(e_first, e_last):
            return slice(e_first * C, (e_last + 1) * C)

        def entries(list_tile, span):
            return list_tile[:, span.start // PER_COL : span.stop // PER_COL]

        offs_sb = lists.tile([P, S // PER_COL], U16, name="offs_sb")
        pos1_sb = lists.tile([P, T // PER_COL], U16, name="pos1_sb")
        pos2_sb = lists.tile([P, T // PER_COL], U16, name="pos2_sb")
        dy_w = keep.tile([P, WORD_WINDOW], I32, name="dy_w")
        dy_s = keep.tile([P, BYTE_WINDOW], U8, name="dy_s")
        gate_rows = keep.tile([P, S], F32, name="gate_rows")
        ident = keep.tile([P, P], F32, name="ident")

        nc.vector.memset(dy_s[:].bitcast(I32), 0)
        nc.vector.memset(dy_w[:, T:WORD_WINDOW], 0)
        nc.sync.dma_start(dy_w[:, 0:T], dy_words[0].rearrange("p t d -> p (t d)").bitcast(I32))
        nc.sync.dma_start(offs_sb[:], offs)
        make_identity(nc, ident[:])

        raw = {}

        def load_w(chunk, experts):
            k0 = sum(CHUNKS[:chunk])
            for e in experts:
                raw[chunk, e] = sbuf(raw_tag(chunk, e), [P, PACK, CHUNKS[chunk]], F32)
                rows = w[e, :, k0 : k0 + CHUNKS[chunk]]
                nc.sync.dma_start(raw[chunk, e][:], rows.rearrange("(p j) k -> p j k", j=PACK))

        load_w(0, range(0, 3))
        for q in range(4):
            nc.sync.dma_start(dy_s[32 * q : 32 * q + 4, 0:T].bitcast(I32), dy_scales[0, 4 * q : 4 * q + 4, :].bitcast(I32))
        load_w(0, range(3, E))
        nc.sync.dma_start(gate_rows[:], gate[0:P, :])
        nc.sync.dma_start(pos1_sb[:], pos1)
        nc.sync.dma_start(pos2_sb[:], pos2)
        for chunk in range(1, len(CHUNKS)):
            load_w(chunk, range(E))

        g_w = keep.tile([P, S], U32, name="g_w", align_bytes=64)
        g_s = keep.tile([P, S], U8, name="g_s", align_bytes=64)
        nc.vector.tensor_copy(g_w[:], dy_w[:].bitcast(U32).indirect(offs_sb[:]))
        for experts in PAIRS:
            cols = slots(experts[0], experts[-1])
            nc.vector.tensor_copy(g_s[:, cols], dy_s[:].indirect(entries(offs_sb, cols)))

        codes = {}
        scales = {}

        def round_and_quantise(chunk, experts):
            kw = CHUNKS[chunk]
            width = len(experts) * kw
            rounded = sbuf(f"rounded{chunk}_{experts[-1]}", [P, width, PACK], BF16)
            words = sbuf(f"codes{chunk}_{experts[-1]}", [P, width], U32)
            plane = sbuf(f"scales{chunk}_{experts[-1]}", [P, width], U8)
            for place, e in enumerate(experts):
                cols = slice(place * kw, (place + 1) * kw)
                nc.scalar.activation(
                    rounded[:, cols, :].rearrange("p (c i) t -> p c t i", i=4),
                    raw[chunk, e][:].rearrange("p t (c i) -> p c t i", i=4),
                    COPY,
                )
                codes[chunk, e] = words[:, cols]
                scales[chunk, e] = plane[:, cols]
            for lo, hi in quantise_pieces(width):
                nc.vector.quantize_mx(
                    out=words[:, lo:hi].bitcast(FP8X4),
                    scales=plane[:, lo:hi],
                    in_=rounded[:, lo:hi, :].rearrange("p k t -> p (k t)"),
                )

        def product(dst, still_words, still_scales, moving_words, moving_scales):
            nc.tensor.matmul_mx(
                out=dst,
                lhsT=still_words.bitcast(FP8X4),
                lhsT_scale=still_scales,
                rhs=moving_words.bitcast(FP8X4),
                rhs_scale=moving_scales,
                start=True,
                stop=True,
            )

        def direct_chunk(chunk, dx):
            for experts in PAIRS:
                cols = slots(experts[0], experts[-1])
                for b in range(len(dx)):
                    bank = next_bank([P, BANK])
                    for place, e in enumerate(experts):
                        product(bank[:, slots(place, place)], codes[chunk, e][:, block(b)], scales[chunk, e][:, block(b)], g_w[:, slots(e, e)], g_s[:, slots(e, e)])
                    nc.vector.tensor_tensor(dx[b][:, cols], bank[:, 0 : len(experts) * C], gate_rows[:, cols], MULT)

        def turned_chunk(dx, scaled):
            fills = [range(lo, min(lo + PER_BANK, SLOT_BLOCKS)) for lo in range(0, SLOT_BLOCKS, PER_BANK)]
            gate_cols = sbuf("gate_cols", [P, SLOT_BLOCKS], F32)
            for fill in fills:
                bank = next_bank([P, PER_BANK, P])
                for j in fill:
                    nc.tensor.transpose(bank[:, j - fill.start, :], gate_rows[:, block(j)], ident[:])
                nc.scalar.copy(gate_cols[:, fill.start : fill.stop], bank[:, 0 : len(fill), 0])
            for b in range(len(dx)):
                for fill in fills:
                    bank = next_bank([P, PER_BANK, P])
                    for j in fill:
                        e = j * P // C
                        product(bank[:, j - fill.start, :], g_w[:, block(j)], g_s[:, block(j)], codes[LAST, e][:, block(b)], scales[LAST, e][:, block(b)])
                    for j in fill:
                        nc.scalar.activation(scaled[:, b, j, :], bank[:, j - fill.start, :], COPY, scale=gate_cols[:, j : j + 1])
                for fill in fills:
                    bank = next_bank([P, BANK])
                    for j in fill:
                        nc.tensor.transpose(bank[:, block(j - fill.start)], scaled[:, b, j, :], ident[:])
                    nc.scalar.copy(dx[b][:, fill.start * P : fill.stop * P], bank[:, 0 : len(fill) * P])

        def combine(chunk, first_block, dx, sums):
            parts = 1 if chunk == MIDDLE else 2
            halves = [slice(part * T // parts, (part + 1) * T // parts) for part in range(parts)]
            first = []
            for b in range(len(dx)):
                picked = sbuf(f"first{first_block + b}", [P, T], F32)
                for toks in halves:
                    nc.vector.tensor_copy(picked[:, toks], dx[b][:].indirect(entries(pos1_sb, toks)))
                first.append(picked)
            for b in range(len(dx)):
                rows = block(first_block + b)
                is_final = rows.stop == K
                for toks in halves:
                    nc.vector.tensor_tensor(sums[:, b, toks], dx[b][:].indirect(entries(pos2_sb, toks)), first[b][:, toks], ADD)
                    if is_final:
                        nc.sync.dma_start(out[rows, toks], sums[:, b, toks])
                if not is_final:
                    nc.sync.dma_start(out[rows, :], sums[:, b, :])

        def chunk_results(chunk):
            first_block = sum(CHUNKS[:chunk]) // P
            return first_block, [sbuf(f"dx{first_block + b}", [P, S], F32) for b in range(CHUNKS[chunk] // P)]

        for experts in GROUPS[0]:
            round_and_quantise(0, experts)

        first_block, dx = chunk_results(0)
        direct_chunk(0, dx)
        for experts in GROUPS[MIDDLE]:
            round_and_quantise(MIDDLE, experts)
        combine(0, first_block, dx, sbuf("sums0", [P, len(dx), T], F32))

        first_block, dx = chunk_results(MIDDLE)
        direct_chunk(MIDDLE, dx)
        for experts in GROUPS[LAST]:
            round_and_quantise(LAST, experts)
        sums_cols = len(dx) * T
        scaled_cols = (CHUNKS[LAST] // P) * S
        after_rounding = sbuf("after_rounding", [P, sums_cols + scaled_cols], F32)
        combine(MIDDLE, first_block, dx, after_rounding[:, 0:sums_cols].rearrange("p (b t) -> p b t", t=T))

        first_block, dx = chunk_results(LAST)
        turned_chunk(dx, after_rounding[:, sums_cols : sums_cols + scaled_cols].rearrange("p (b j k) -> p b j k", j=SLOT_BLOCKS, k=P))
        combine(LAST, first_block, dx, sbuf("sums2", [P, len(dx), T], F32))
